import numpy as np
import ml_dtypes


def mxq(x, axis, fmt="e4m3"):
    dtype, down = {"e4m3": (ml_dtypes.float8_e4m3fn, 7), "e5m2": (ml_dtypes.float8_e5m2, 14)}[fmt]
    v = np.moveaxis(np.asarray(x, np.float32).astype(ml_dtypes.bfloat16).astype(np.float64), axis, -1)
    blocks = v.reshape(v.shape[:-1] + (-1, 32))
    amax = np.abs(blocks).max(-1, keepdims=True)
    byte = np.maximum(np.where(amax > 0, np.frexp(amax)[1] - 1 + 127, 0) - down, 1)
    scale = np.exp2(byte - 127.0)
    codes = (blocks / scale).astype(np.float32).astype(dtype).astype(np.float64)
    return np.moveaxis((codes * scale).reshape(v.shape), -1, axis)


WIDE = False


def mx_kscale(k):
    if not WIDE:
        return np.ones(k)
    levels = np.array([10, -10, 5, -5, 0])
    if k % 512:
        return np.exp2(np.random.permutation(np.resize(levels, k // 32))).repeat(32)
    a = np.empty((k // 512, 16))
    for p in range(k // 512):
        a[p, :8] = np.random.permutation(np.resize(levels, 8))
        for g in range(8):
            far = levels[np.abs(levels - a[p, g]) >= 10]
            a[p, g + 8] = far[np.random.randint(len(far))]
    return np.exp2(a.ravel()).repeat(32)


def f64(x):
    return np.asarray(x).astype(np.float64)


def striped(idx):
    return np.tile(idx.reshape(-1, 16).T, (8, 1)).astype(np.uint16)


def unstriped(offs):
    return offs[:16].T.reshape(-1).astype(np.int64)


E2M1 = np.array([0.0, 0.5, 1.0, 1.5, 2.0, 3.0, 4.0, 6.0, -0.0, -0.5, -1.0, -1.5, -2.0, -3.0, -4.0, -6.0])


def pack_weight(w, fmt):
    k, n = w.shape
    w = f64(np.asarray(w, np.float32).astype(ml_dtypes.bfloat16)).reshape(k // 32, 32, n)
    amax = np.abs(w).max(1)
    if fmt == "e4m3":
        byte = np.frexp(amax)[1] - 1 + 127 - 7
    else:
        mant, ex = np.frexp(amax / 6.0)
        byte = np.where(mant > 0.5, ex, ex - 1) + 127
    byte = np.clip(np.where(amax > 0, byte, 1), 1, 254)
    scaled = (w * np.exp2(127.0 - byte)[:, None, :]).reshape(k, n).astype(np.float32)
    by_word = np.ascontiguousarray(scaled.reshape(k // 512, 128, 4, n).transpose(0, 1, 3, 2))
    if fmt == "e4m3":
        words = by_word.astype(ml_dtypes.float8_e4m3fn).view(np.uint8)
    else:
        c = by_word.astype(ml_dtypes.float4_e2m1fn).view(np.uint8) & 0xF
        words = (c[..., 0::2] | (c[..., 1::2] << 4)).reshape(k // 512, 128, 2 * n)
    return np.ascontiguousarray(words), np.ascontiguousarray(byte.astype(np.uint8).reshape(k // 512, 16, n))


def unpack_weight(words, scales, fmt):
    g, _, n = scales.shape
    words = np.ascontiguousarray(words).reshape(g, 128, n, -1)
    if fmt == "e4m3":
        vals = words.view(ml_dtypes.float8_e4m3fn).astype(np.float64)
    else:
        nib = np.empty((g, 128, n, 4), np.uint8)
        nib[..., 0::2] = words & 0xF
        nib[..., 1::2] = words >> 4
        vals = E2M1[nib]
    vals = vals * np.repeat(np.exp2(scales.astype(np.float64) - 127.0), 8, axis=1)[..., None]
    return vals.transpose(0, 1, 3, 2).reshape(g * 512, n)


def gelu(v):
    return 0.5 * v * (1.0 + np.tanh(np.sqrt(2.0 / np.pi) * (v + 0.044715 * v**3)))


K, T, E, C, N = 1536, 768, 12, 256, 128
TOP = 4


def by_expert(wq, xq):
    return np.concatenate([wq[e].T @ xq[:, e * C:(e + 1) * C] for e in range(E)], axis=1)


def setup_inputs():
    n = np.random.standard_normal
    s = mx_kscale(K)[:, None]
    deal = np.repeat(np.arange(E), C).reshape(TOP, T)[:, np.random.permutation(T)]
    deal = np.take_along_axis(deal, np.argsort(np.random.rand(TOP, T), axis=0), axis=0)
    for _ in range(8):
        s_, t_ = np.random.permutation(T).reshape(2, -1); r = np.random.randint(TOP, size=T // 2); x, y = deal[r, s_].copy(), deal[r, t_].copy()
        ok = ~((deal[:, s_] == y).any(0) | (deal[:, t_] == x).any(0)); deal[r[ok], s_[ok]] = y[ok]; deal[r[ok], t_[ok]] = x[ok]
    order = np.lexsort((np.random.rand(TOP * T), deal.reshape(-1)))
    slot_token = order % T; pos = np.empty(TOP * T, np.int64); pos[order] = np.arange(TOP * T); pos = pos.reshape(TOP, T)
    g = np.random.uniform(0.5, 1.5, (TOP, T)); g = g / g.sum(0)
    x = pack_weight(n((K, T)) * s, "e4m3")
    return {
        "x_words": x[0],
        "x_scales": x[1],
        "w": (n((E + 1, K, N)) / np.sqrt(K) / s[None]).astype(np.float32),
        "b": (0.3 * n((N, E + 1))).astype(np.float32),
        "gate": np.stack([np.tile(r, (N, 1)) for r in g]).astype(np.float32),
        "offs": striped(slot_token),
        "pos1": striped(pos[0]),
        "pos2": striped(pos[1]),
        "pos3": striped(pos[2]),
        "pos4": striped(pos[3]),
    }


def reference(x_words, x_scales, w, b, gate, offs, pos1, pos2, pos3, pos4):
    idx = unstriped(offs)
    wq = mxq(f64(w), 1, "e4m3")
    xs = unpack_weight(x_words, x_scales, "e4m3")
    ys = gelu((wq[E].T @ xs) + f64(b)[:, E:])
    xq = unpack_weight(x_words, x_scales, "e4m3")[:, idx]
    y = by_expert(wq, xq)
    y = gelu(y + np.repeat(f64(b)[:, :E], C, axis=1))
    return ys + sum(f64(gate[r]) * y[:, unstriped(p)] for r, p in enumerate((pos1, pos2, pos3, pos4)))

@@ -1,0 +1,182 @@
+from contextlib import ExitStack
+
+import concourse.mybir as mybir
+
+K, T, E, C, N = 1536, 768, 12, 256, 128
+TOP = 4
+S = E * C
+FLOPS = 2 * K * N * (S + T)
+
+F32 = mybir.dt.float32
+BF16 = mybir.dt.bfloat16
+I32 = mybir.dt.int32
+U32 = mybir.dt.uint32
+U16 = mybir.dt.uint16
+U8 = mybir.dt.uint8
+FP8X4 = mybir.dt.float8_e4m3fn_x4
+GELU = mybir.ActivationFunctionType.Gelu_apprx_tanh
+MULT = mybir.AluOpType.mult
+ADD = mybir.AluOpType.add
+
+P = 128
+PACK = 4
+PASSES = K // (P * PACK)
+CHUNK = 2 * C
+LANES = 16
+
+
+def tile_moe_shr_lin_gelu_kernel(
+    tc, x_words, x_scales, w, b, gate, offs, pos1, pos2, pos3, pos4, out
+):
+    nc = tc.nc
+    with ExitStack() as ctx:
+        lists = ctx.enter_context(tc.tile_pool(name="lists", bufs=1))
+        held = ctx.enter_context(tc.tile_pool(name="held", bufs=1))
+        psum = ctx.enter_context(tc.psum_pool(name="psum", bufs=1))
+
+        slot_list = lists.tile([P, S // LANES], U16, name="slot_list")
+        back_lists = [lists.tile([P, T // LANES], U16, name="back_list%d" % r) for r in range(TOP)]
+        tok_words = [held.tile([P, T], I32, name="tok_words%d" % a, align_bytes=64) for a in range(PASSES)]
+        tok_scales = held.tile([P, T], U8, name="tok_scales", align_bytes=64)
+        w_raw = [held.tile([P, PASSES, PACK, N], F32, name="w_raw%d" % e, tag="raw%d" % e, align_bytes=64) for e in range(E + 1)]
+        w_codes = [held.tile([P, PASSES * N], U32, name="w_codes%d" % e, align_bytes=64) for e in range(E + 1)]
+        w_scales = [held.tile([P, PASSES * N], U8, name="w_scales%d" % e, align_bytes=64) for e in range(E + 1)]
+        bias = held.tile([P, E + 1], F32, name="bias")
+        gates = held.tile([P, TOP, T], F32, name="gates")
+        y = held.tile([P, S], F32, name="y")
+        total = held.tile([P, T], F32, name="total")
+        parts = [held.tile([P, T], F32, name="part%d" % r) for r in range(TOP)]
+        warm = held.tile([P, 1], F32, name="warm")
+        warm_out = held.tile([P, 1], F32, name="warm_out")
+
+        def load_words(a):
+            nc.sync.dma_start(tok_words[a][:], x_words[a].rearrange("p t r -> p (t r)").bitcast(I32))
+
+        def load_weight(e):
+            nc.sync.dma_start(w_raw[e][:], w[e].rearrange("(a p j) n -> p a j n", a=PASSES, j=PACK))
+
+        nc.vector.memset(tok_scales[:].bitcast(I32), 0)
+        nc.vector.memset(warm[:], 0.0)
+        nc.sync.dma_start(slot_list[:], offs)
+        load_words(0)
+        for q in range(4):
+            nc.scalar.dma_start(
+                tok_scales[32 * q : 32 * q + 4 * PASSES, :].bitcast(I32),
+                x_scales[:, 4 * q : 4 * q + 4, :].bitcast(I32),
+            )
+        nc.scalar.activation(warm_out[:], warm[:], GELU)
+        load_words(1)
+        load_weight(0)
+        load_words(2)
+        for e in range(1, E + 1):
+            load_weight(e)
+        nc.sync.dma_start(bias[:], b)
+        for tile, pos in zip(back_lists, (pos1, pos2, pos3, pos4)):
+            nc.sync.dma_start(tile[:], pos)
+        nc.sync.dma_start(gates[:], gate.rearrange("r n t -> n r t"))
+
+        def quantize_weight(e):
+            w_bf = held.tile([P, PASSES, N, PACK], BF16, name="w_bf%d" % e, align_bytes=64)
+            nc.scalar.copy(
+                w_bf[:].rearrange("p a (c i) j -> p a c j i", i=4),
+                w_raw[e][:].rearrange("p a j (c i) -> p a c j i", i=4),
+            )
+            flat = w_bf[:].rearrange("p a n j -> p (a n j)")
+            for lo, hi in ((0, 2 * N), (2 * N, 3 * N)):
+                nc.vector.quantize_mx(
+                    out=w_codes[e][:, lo:hi].bitcast(FP8X4),
+                    scales=w_scales[e][:, lo:hi],
+                    in_=flat[:, PACK * lo : PACK * hi],
+                )
+
+        def multiply(e, acc, words, scales, cols):
+            for a in range(PASSES):
+                nc.tensor.matmul_mx(
+                    out=acc,
+                    lhsT=w_codes[e][:, a * N : (a + 1) * N].bitcast(FP8X4),
+                    lhsT_scale=w_scales[e][:, a * N : (a + 1) * N],
+                    rhs=words[a][:, cols].bitcast(FP8X4),
+                    rhs_scale=scales[4 * a : P, cols],
+                    start=(a == 0),
+                    stop=(a == PASSES - 1),
+                )
+
+        def offsets(lo, hi):
+            return slot_list[:, lo // LANES : hi // LANES]
+
+        chunks = S // CHUNK
+        slot_words, slot_scales = {}, {}
+
+        def gather_words(c, tag):
+            tile = held.tile([P, PASSES, CHUNK], U32, name="slot_words%d" % c, tag=tag, align_bytes=64)
+            slot_words[c] = [tile[:, a, :] for a in range(PASSES)]
+
+        def gather_pass(c, a, p0=0, p1=CHUNK):
+            nc.vector.tensor_copy(
+                slot_words[c][a][:, p0:p1],
+                tok_words[a][:].bitcast(U32).indirect(offsets(c * CHUNK + p0, c * CHUNK + p1)),
+            )
+
+        def gather_scales(c, tag):
+            slot_scales[c] = held.tile([P, CHUNK], U8, name="slot_scales%d" % c, tag=tag, align_bytes=64)
+            nc.vector.tensor_copy(slot_scales[c][:], tok_scales[:].indirect(offsets(c * CHUNK, (c + 1) * CHUNK)))
+
+        words_after = {2: 2, 4: 3, 6: 4, 11: 5}
+        scales_after = {0: 0, 1: 1, 3: 2, 5: 3, 7: 4, 8: 5}
+        for c in range(2):
+            gather_words(c, "first_words%d" % c)
+        for a in range(PASSES):
+            for c in range(2):
+                gather_pass(c, a)
+        for e in range(E + 1):
+            quantize_weight(e)
+            if e in scales_after:
+                gather_scales(scales_after[e], "raw%d" % e)
+            if e in words_after:
+                c = words_after[e]
+                gather_words(c, "raw%d" % e)
+                gather_pass(c, 0)
+                gather_pass(c, 1)
+                if c < chunks - 1:
+                    gather_pass(c, 2)
+                else:
+                    gather_pass(c, 2, 0, C)
+                    gather_pass(c, 2, C, CHUNK)
+
+        sums = []
+        for c in range(chunks - 1):
+            bank = psum.tile([P, CHUNK], F32, name="bank%d" % c)
+            sums += [bank[:, 0:C], bank[:, C:CHUNK]]
+        for e in (E - 2, E - 1):
+            bank = psum.tile([P, C], F32, name="bank_expert%d" % e)
+            sums.append(bank[:])
+        for e in range(E):
+            c, h = divmod(e, 2)
+            multiply(e, sums[e], slot_words[c], slot_scales[c], slice(h * C, (h + 1) * C))
+        for e in range(E):
+            nc.scalar.activation(y[:, e * C : (e + 1) * C], sums[e], GELU, bias=bias[:, e : e + 1])
+
+        for lo, hi, tag in ((0, 512, "bank_shared"), (512, T, "bank0")):
+            acc_shared = psum.tile([P, hi - lo], F32, name="acc_shared%d" % lo, tag=tag)
+            multiply(E, acc_shared[:], tok_words, tok_scales, slice(lo, hi))
+            nc.scalar.activation(total[:, lo:hi], acc_shared[:], GELU, bias=bias[:, E : E + 1])
+
+        def fetch(r, lo, hi):
+            nc.vector.tensor_tensor(
+                parts[r][:, lo:hi], y[:].indirect(back_lists[r][:, lo // LANES : hi // LANES]), gates[:, r, lo:hi], MULT
+            )
+
+        def add(r, lo, hi):
+            nc.vector.tensor_tensor(total[:, lo:hi], total[:, lo:hi], parts[r][:, lo:hi], ADD)
+
+        fetch(0, 0, T)
+        fetch(1, 0, T)
+        add(0, 0, T)
+        fetch(2, 0, T)
+        add(1, 0, T)
+        fetch(3, 0, 512)
+        add(2, 0, T)
+        fetch(3, 512, T)
+        for lo, hi in ((0, 512), (512, T)):
+            add(3, lo, hi)
+            nc.sync.dma_start(out[:, lo:hi], total[:, lo:hi])

@@ -1,6 +1,7 @@
 from contextlib import ExitStack
 
 import concourse.mybir as mybir
+from concourse.masks import make_identity
 
 K, T, E, C, N = 1536, 768, 12, 256, 128
 TOP = 4
@@ -21,7 +22,8 @@ ADD = mybir.AluOpType.add
 P = 128
 PACK = 4
 PASSES = K // (P * PACK)
-CHUNK = 2 * C
+WIDE = 2048
+HALF = S // 2
 LANES = 16
 
 
@@ -36,11 +38,15 @@ def tile_moe_shr_lin_gelu_kernel(
 
         slot_list = lists.tile([P, S // LANES], U16, name="slot_list")
         back_lists = [lists.tile([P, T // LANES], U16, name="back_list%d" % r) for r in range(TOP)]
-        tok_words = [held.tile([P, T], I32, name="tok_words%d" % a, align_bytes=64) for a in range(PASSES)]
-        tok_scales = held.tile([P, T], U8, name="tok_scales", align_bytes=64)
+        tok_words = held.tile([P, (PASSES - 1) * T + WIDE], I32, name="tok_words", align_bytes=64)
+        tok_scales = held.tile([P, WIDE], U8, name="tok_scales", align_bytes=64)
         w_raw = [held.tile([P, PASSES, PACK, N], F32, name="w_raw%d" % e, tag="raw%d" % e, align_bytes=64) for e in range(E + 1)]
-        w_codes = [held.tile([P, PASSES * N], U32, name="w_codes%d" % e, align_bytes=64) for e in range(E + 1)]
-        w_scales = [held.tile([P, PASSES * N], U8, name="w_scales%d" % e, align_bytes=64) for e in range(E + 1)]
+        w_bf = held.tile([P, (E + 1) * PASSES, N, PACK], BF16, name="w_bf", align_bytes=64)
+        w_codes = held.tile([P, (E + 1) * PASSES * N], U32, name="w_codes", align_bytes=64)
+        w_scales = held.tile([P, (E + 1) * PASSES * N], U8, name="w_scales", align_bytes=64)
+        identity = held.tile([P, P], F32, name="identity")
+        shared = held.tile([P, T], F32, name="shared")
+        turned = held.tile([P, T], F32, name="turned")
         bias = held.tile([P, E + 1], F32, name="bias")
         gates = held.tile([P, TOP, T], F32, name="gates")
         y = held.tile([P, S], F32, name="y")
@@ -50,53 +56,55 @@ def tile_moe_shr_lin_gelu_kernel(
         warm_out = held.tile([P, 1], F32, name="warm_out")
 
         def load_words(a):
-            nc.sync.dma_start(tok_words[a][:], x_words[a].rearrange("p t r -> p (t r)").bitcast(I32))
+            nc.sync.dma_start(tok_words[:, a * T : (a + 1) * T], x_words[a].rearrange("p t r -> p (t r)").bitcast(I32))
 
         def load_weight(e):
             nc.sync.dma_start(w_raw[e][:], w[e].rearrange("(a p j) n -> p a j n", a=PASSES, j=PACK))
 
-        nc.vector.memset(tok_scales[:].bitcast(I32), 0)
+        nc.vector.memset(tok_scales[:, 0:T].bitcast(I32), 0)
         nc.vector.memset(warm[:], 0.0)
+        nc.vector.memset(tok_scales[:, T:WIDE].bitcast(I32), 0)
+        nc.vector.memset(tok_words[:, PASSES * T :], 0)
+        make_identity(nc, identity[:])
         nc.sync.dma_start(slot_list[:], offs)
         load_words(0)
         for q in range(4):
             nc.scalar.dma_start(
-                tok_scales[32 * q : 32 * q + 4 * PASSES, :].bitcast(I32),
+                tok_scales[32 * q : 32 * q + 4 * PASSES, 0:T].bitcast(I32),
                 x_scales[:, 4 * q : 4 * q + 4, :].bitcast(I32),
             )
         nc.scalar.activation(warm_out[:], warm[:], GELU)
         load_words(1)
-        load_weight(0)
         load_words(2)
-        for e in range(1, E + 1):
+        for e in range(E + 1):
             load_weight(e)
         nc.sync.dma_start(bias[:], b)
         for tile, pos in zip(back_lists, (pos1, pos2, pos3, pos4)):
             nc.sync.dma_start(tile[:], pos)
         nc.sync.dma_start(gates[:], gate.rearrange("r n t -> n r t"))
 
-        def quantize_weight(e):
-            w_bf = held.tile([P, PASSES, N, PACK], BF16, name="w_bf%d" % e, align_bytes=64)
+        def round_weight(e):
             nc.scalar.copy(
-                w_bf[:].rearrange("p a (c i) j -> p a c j i", i=4),
+                w_bf[:, e * PASSES : (e + 1) * PASSES].rearrange("p a (c i) j -> p a c j i", i=4),
                 w_raw[e][:].rearrange("p a j (c i) -> p a c j i", i=4),
             )
-            flat = w_bf[:].rearrange("p a n j -> p (a n j)")
-            for lo, hi in ((0, 2 * N), (2 * N, 3 * N)):
-                nc.vector.quantize_mx(
-                    out=w_codes[e][:, lo:hi].bitcast(FP8X4),
-                    scales=w_scales[e][:, lo:hi],
-                    in_=flat[:, PACK * lo : PACK * hi],
-                )
 
-        def multiply(e, acc, words, scales, cols):
+        w_flat = w_bf[:].rearrange("p a n j -> p (a n j)")
+
+        def quantize(lo, hi):
+            nc.vector.quantize_mx(
+                out=w_codes[:, lo:hi].bitcast(FP8X4), scales=w_scales[:, lo:hi], in_=w_flat[:, PACK * lo : PACK * hi]
+            )
+
+        def multiply(e, acc, words, scales):
             for a in range(PASSES):
+                cols = slice((e * PASSES + a) * N, (e * PASSES + a + 1) * N)
                 nc.tensor.matmul_mx(
                     out=acc,
-                    lhsT=w_codes[e][:, a * N : (a + 1) * N].bitcast(FP8X4),
-                    lhsT_scale=w_scales[e][:, a * N : (a + 1) * N],
-                    rhs=words[a][:, cols].bitcast(FP8X4),
-                    rhs_scale=scales[4 * a : P, cols],
+                    lhsT=w_codes[:, cols].bitcast(FP8X4),
+                    lhsT_scale=w_scales[:, cols],
+                    rhs=words[a].bitcast(FP8X4),
+                    rhs_scale=scales[a],
                     start=(a == 0),
                     stop=(a == PASSES - 1),
                 )
@@ -104,79 +112,109 @@ def tile_moe_shr_lin_gelu_kernel(
         def offsets(lo, hi):
             return slot_list[:, lo // LANES : hi // LANES]
 
-        chunks = S // CHUNK
         slot_words, slot_scales = {}, {}
 
-        def gather_words(c, tag):
-            tile = held.tile([P, PASSES, CHUNK], U32, name="slot_words%d" % c, tag=tag, align_bytes=64)
-            slot_words[c] = [tile[:, a, :] for a in range(PASSES)]
+        def gather_words(a, lo, hi, dst, width):
+            window = tok_words[:, a * T : a * T + width].bitcast(U32)
+            nc.vector.tensor_copy(dst, window.indirect(offsets(lo, hi)))
+            for e in range(lo // C, hi // C):
+                slot_words[(e, a)] = dst[:, e * C - lo : (e + 1) * C - lo]
 
-        def gather_pass(c, a, p0=0, p1=CHUNK):
-            nc.vector.tensor_copy(
-                slot_words[c][a][:, p0:p1],
-                tok_words[a][:].bitcast(U32).indirect(offsets(c * CHUNK + p0, c * CHUNK + p1)),
-            )
+        def gather_scales(lo, hi, tag):
+            tile = held.tile([P, hi - lo], U8, name="slot_scales%d" % lo, tag=tag, align_bytes=64)
+            nc.vector.tensor_copy(tile[:], tok_scales[:].indirect(offsets(lo, hi)))
+            for e in range(lo // C, hi // C):
+                for a in range(PASSES):
+                    slot_scales[(e, a)] = tile[4 * a : P, e * C - lo : (e + 1) * C - lo]
 
-        def gather_scales(c, tag):
-            slot_scales[c] = held.tile([P, CHUNK], U8, name="slot_scales%d" % c, tag=tag, align_bytes=64)
-            nc.vector.tensor_copy(slot_scales[c][:], tok_scales[:].indirect(offsets(c * CHUNK, (c + 1) * CHUNK)))
+        def words_tile(name, width, tag):
+            return held.tile([P, width], U32, name=name, tag=tag, align_bytes=64)
 
-        words_after = {2: 2, 4: 3, 6: 4, 11: 5}
-        scales_after = {0: 0, 1: 1, 3: 2, 5: 3, 7: 4, 8: 5}
-        for c in range(2):
-            gather_words(c, "first_words%d" % c)
-        for a in range(PASSES):
-            for c in range(2):
-                gather_pass(c, a)
+        first = words_tile("words_0a", HALF, "words_0a")
+        gather_words(0, 0, 2 * C, first[:, 0 : 2 * C], T)
+        gather_words(0, 2 * C, HALF, first[:, 2 * C : HALF], 2 * T)
+        gather_words(1, 0, HALF, words_tile("words_1a", HALF, "words_1a")[:], WIDE)
+        step = WIDE // PACK
+        done = 0
         for e in range(E + 1):
-            quantize_weight(e)
-            if e in scales_after:
-                gather_scales(scales_after[e], "raw%d" % e)
-            if e in words_after:
-                c = words_after[e]
-                gather_words(c, "raw%d" % e)
-                gather_pass(c, 0)
-                gather_pass(c, 1)
-                if c < chunks - 1:
-                    gather_pass(c, 2)
-                else:
-                    gather_pass(c, 2, 0, C)
-                    gather_pass(c, 2, C, CHUNK)
+            round_weight(e)
+            while e < E and done + step <= (e + 1) * PASSES * N:
+                quantize(done, done + step)
+                done += step
+            tag = "raw%d" % e
+            if e == 1:
+                gather_words(2, 0, HALF, words_tile("words_2a", HALF, tag)[:], WIDE)
+            if e == 3:
+                gather_scales(0, HALF, tag)
+            if e == 6:
+                gather_scales(HALF, S, tag)
+            if e == 7:
+                gather_words(0, HALF, S, words_tile("words_0b", HALF, tag)[:], WIDE)
+            if e == 10:
+                gather_words(2, HALF, 10 * C, words_tile("words_2b", 4 * C, tag)[:], WIDE)
+            if e == 11:
+                gather_words(1, HALF, 10 * C, words_tile("words_1b", 4 * C, tag)[:], WIDE)
+            if e == 12:
+                last = words_tile("words_last", 4 * C, tag)
+                gather_words(1, 10 * C, S, last[:, 0 : 2 * C], T)
+                gather_words(2, 10 * C, 11 * C, last[:, 2 * C : 3 * C], T)
+                gather_words(2, 11 * C, S, last[:, 3 * C : 4 * C], T)
+        quantize(done, done + 2 * N)
+        quantize(done + 2 * N, done + 3 * N)
 
         sums = []
-        for c in range(chunks - 1):
-            bank = psum.tile([P, CHUNK], F32, name="bank%d" % c)
-            sums += [bank[:, 0:C], bank[:, C:CHUNK]]
+        for c in range(E // 2 - 1):
+            bank = psum.tile([P, 2 * C], F32, name="bank%d" % c)
+            sums += [bank[:, 0:C], bank[:, C : 2 * C]]
         for e in (E - 2, E - 1):
-            bank = psum.tile([P, C], F32, name="bank_expert%d" % e)
+            bank = psum.tile([P, C], F32, name="bank%d" % (e - 5))
             sums.append(bank[:])
         for e in range(E):
-            c, h = divmod(e, 2)
-            multiply(e, sums[e], slot_words[c], slot_scales[c], slice(h * C, (h + 1) * C))
+            multiply(e, sums[e], [slot_words[(e, a)] for a in range(PASSES)], [slot_scales[(e, a)] for a in range(PASSES)])
         for e in range(E):
             nc.scalar.activation(y[:, e * C : (e + 1) * C], sums[e], GELU, bias=bias[:, e : e + 1])
 
-        for lo, hi, tag in ((0, 512, "bank_shared"), (512, T, "bank0")):
+        pieces = ((0, 512, "bank7"), (512, T, "bank0"))
+        for lo, hi, tag in pieces:
             acc_shared = psum.tile([P, hi - lo], F32, name="acc_shared%d" % lo, tag=tag)
-            multiply(E, acc_shared[:], tok_words, tok_scales, slice(lo, hi))
-            nc.scalar.activation(total[:, lo:hi], acc_shared[:], GELU, bias=bias[:, E : E + 1])
+            multiply(
+                E,
+                acc_shared[:],
+                [tok_words[:, a * T + lo : a * T + hi] for a in range(PASSES)],
+                [tok_scales[4 * a : P, lo:hi] for a in range(PASSES)],
+            )
+            nc.scalar.activation(shared[:, lo:hi], acc_shared[:], GELU, bias=bias[:, E : E + 1])
 
         def fetch(r, lo, hi):
             nc.vector.tensor_tensor(
                 parts[r][:, lo:hi], y[:].indirect(back_lists[r][:, lo // LANES : hi // LANES]), gates[:, r, lo:hi], MULT
             )
 
-        def add(r, lo, hi):
-            nc.vector.tensor_tensor(total[:, lo:hi], total[:, lo:hi], parts[r][:, lo:hi], ADD)
+        blocks = T // P
+        turned_sums = [psum.tile([P, P], F32, name="turned_sum%d" % j, tag="bank%d" % (j + 1)) for j in range(blocks)]
+
+        def add_turned(src, js, start, stop):
+            for j in js:
+                nc.tensor.matmul(
+                    turned_sums[j][:], src[:, j * P : (j + 1) * P], identity[:], start=start, stop=stop, is_transpose=True
+                )
 
         fetch(0, 0, T)
+        add_turned(parts[0], range(blocks), True, False)
+        add_turned(shared, range(blocks), False, False)
         fetch(1, 0, T)
-        add(0, 0, T)
-        fetch(2, 0, T)
-        add(1, 0, T)
-        fetch(3, 0, 512)
-        add(2, 0, T)
-        fetch(3, 512, T)
-        for lo, hi in ((0, 512), (512, T)):
-            add(3, lo, hi)
+        add_turned(parts[1], range(blocks), False, False)
+        for j0 in (0, blocks // 2):
+            js = range(j0, j0 + blocks // 2)
+            fetch(2, js.start * P, js.stop * P)
+            add_turned(parts[2], js, False, True)
+            for j in js:
+                nc.scalar.copy(turned[:, j * P : (j + 1) * P], turned_sums[j][:])
+        for lo, hi, tag in pieces:
+            fetch(3, lo, hi)
+        for lo, hi, tag in pieces:
+            back = psum.tile([P, hi - lo], F32, name="back%d" % lo, tag=tag)
+            for c0 in range(lo, hi, P):
+                nc.tensor.transpose(back[:, c0 - lo : c0 - lo + P], turned[:, c0 : c0 + P], identity[:])
+            nc.vector.tensor_tensor(total[:, lo:hi], back[:], parts[3][:, lo:hi], ADD)
             nc.sync.dma_start(out[:, lo:hi], total[:, lo:hi])

@@ -55,33 +55,39 @@ def tile_moe_shr_lin_gelu_kernel(
         warm = held.tile([P, 1], F32, name="warm")
         warm_out = held.tile([P, 1], F32, name="warm_out")
 
+        def first_word(a):
+            return (PASSES - 1 - a) * T
+
         def load_words(a):
-            nc.sync.dma_start(tok_words[:, a * T : (a + 1) * T], x_words[a].rearrange("p t r -> p (t r)").bitcast(I32))
+            nc.sync.dma_start(tok_words[:, first_word(a) : first_word(a) + T], x_words[a].rearrange("p t r -> p (t r)").bitcast(I32))
 
         def load_weight(e):
             nc.sync.dma_start(w_raw[e][:], w[e].rearrange("(a p j) n -> p a j n", a=PASSES, j=PACK))
 
-        nc.vector.memset(tok_scales[:, 0:T].bitcast(I32), 0)
         nc.vector.memset(warm[:], 0.0)
-        nc.vector.memset(tok_scales[:, T:WIDE].bitcast(I32), 0)
         nc.vector.memset(tok_words[:, PASSES * T :], 0)
+        nc.vector.memset(tok_scales[:].bitcast(I32), 0)
         make_identity(nc, identity[:])
         nc.sync.dma_start(slot_list[:], offs)
         load_words(0)
-        for q in range(4):
-            nc.scalar.dma_start(
-                tok_scales[32 * q : 32 * q + 4 * PASSES, 0:T].bitcast(I32),
-                x_scales[:, 4 * q : 4 * q + 4, :].bitcast(I32),
-            )
         nc.scalar.activation(warm_out[:], warm[:], GELU)
-        load_words(1)
-        load_words(2)
         for e in range(E + 1):
             load_weight(e)
+            if e == 1:
+                for q in range(4):
+                    nc.sync.dma_start(
+                        tok_scales[32 * q : 32 * q + 4 * PASSES, 0:T].bitcast(I32),
+                        x_scales[:, 4 * q : 4 * q + 4, :].bitcast(I32),
+                    )
+            if e == 2:
+                load_words(1)
+            if e == 4:
+                load_words(2)
         nc.sync.dma_start(bias[:], b)
         for tile, pos in zip(back_lists, (pos1, pos2, pos3, pos4)):
             nc.sync.dma_start(tile[:], pos)
-        nc.sync.dma_start(gates[:], gate.rearrange("r n t -> n r t"))
+        for r in range(TOP):
+            nc.sync.dma_start(gates[:, r, :], gate[r])
 
         def round_weight(e):
             nc.scalar.copy(
@@ -113,27 +119,28 @@ def tile_moe_shr_lin_gelu_kernel(
             return slot_list[:, lo // LANES : hi // LANES]
 
         slot_words, slot_scales = {}, {}
+        spans = [(e * C, (e + 1) * C) for e in range(E - 1)] + [(S - C, S - C // 2), (S - C // 2, S)]
 
         def gather_words(a, lo, hi, dst, width):
-            window = tok_words[:, a * T : a * T + width].bitcast(U32)
+            window = tok_words[:, first_word(a) : first_word(a) + width].bitcast(U32)
             nc.vector.tensor_copy(dst, window.indirect(offsets(lo, hi)))
-            for e in range(lo // C, hi // C):
-                slot_words[(e, a)] = dst[:, e * C - lo : (e + 1) * C - lo]
+            for s0, s1 in spans:
+                if lo <= s0 and s1 <= hi:
+                    slot_words[(s0, a)] = dst[:, s0 - lo : s1 - lo]
 
         def gather_scales(lo, hi, tag):
             tile = held.tile([P, hi - lo], U8, name="slot_scales%d" % lo, tag=tag, align_bytes=64)
             nc.vector.tensor_copy(tile[:], tok_scales[:].indirect(offsets(lo, hi)))
-            for e in range(lo // C, hi // C):
-                for a in range(PASSES):
-                    slot_scales[(e, a)] = tile[4 * a : P, e * C - lo : (e + 1) * C - lo]
+            for s0, s1 in spans:
+                if lo <= s0 and s1 <= hi:
+                    for a in range(PASSES):
+                        slot_scales[(s0, a)] = tile[4 * a : P, s0 - lo : s1 - lo]
 
         def words_tile(name, width, tag):
             return held.tile([P, width], U32, name=name, tag=tag, align_bytes=64)
 
-        first = words_tile("words_0a", HALF, "words_0a")
-        gather_words(0, 0, 2 * C, first[:, 0 : 2 * C], T)
-        gather_words(0, 2 * C, HALF, first[:, 2 * C : HALF], 2 * T)
-        gather_words(1, 0, HALF, words_tile("words_1a", HALF, "words_1a")[:], WIDE)
+        gather_words(0, 0, HALF, words_tile("words_0a", HALF, "words_0a")[:], WIDE)
+        gather_words(0, HALF, S, words_tile("words_0b", HALF, "words_0b")[:], WIDE)
         step = WIDE // PACK
         done = 0
         for e in range(E + 1):
@@ -142,23 +149,25 @@ def tile_moe_shr_lin_gelu_kernel(
                 quantize(done, done + step)
                 done += step
             tag = "raw%d" % e
-            if e == 1:
-                gather_words(2, 0, HALF, words_tile("words_2a", HALF, tag)[:], WIDE)
-            if e == 3:
+            if e == 0:
                 gather_scales(0, HALF, tag)
+            if e == 1:
+                gather_words(1, 0, HALF, words_tile("words_1a", HALF, tag)[:], WIDE)
+            if e == 3:
+                gather_words(2, 0, HALF, words_tile("words_2a", HALF, tag)[:], WIDE)
             if e == 6:
                 gather_scales(HALF, S, tag)
-            if e == 7:
-                gather_words(0, HALF, S, words_tile("words_0b", HALF, tag)[:], WIDE)
-            if e == 10:
+            if e == 8:
                 gather_words(2, HALF, 10 * C, words_tile("words_2b", 4 * C, tag)[:], WIDE)
-            if e == 11:
+            if e == 9:
                 gather_words(1, HALF, 10 * C, words_tile("words_1b", 4 * C, tag)[:], WIDE)
-            if e == 12:
-                last = words_tile("words_last", 4 * C, tag)
-                gather_words(1, 10 * C, S, last[:, 0 : 2 * C], T)
-                gather_words(2, 10 * C, 11 * C, last[:, 2 * C : 3 * C], T)
-                gather_words(2, 11 * C, S, last[:, 3 * C : 4 * C], T)
+            if e == 10:
+                gather_words(1, 10 * C, S, words_tile("words_1c", 2 * C, tag)[:], T)
+            if e == 11:
+                last = words_tile("words_2c", 2 * C, tag)
+                gather_words(2, 10 * C, 11 * C, last[:, 0:C], T)
+                gather_words(2, S - C, S - C // 2, last[:, C : C + C // 2], T)
+                gather_words(2, S - C // 2, S, last[:, C + C // 2 : 2 * C], T)
         quantize(done, done + 2 * N)
         quantize(done + 2 * N, done + 3 * N)
 
@@ -166,21 +175,21 @@ def tile_moe_shr_lin_gelu_kernel(
         for c in range(E // 2 - 1):
             bank = psum.tile([P, 2 * C], F32, name="bank%d" % c)
             sums += [bank[:, 0:C], bank[:, C : 2 * C]]
-        for e in (E - 2, E - 1):
-            bank = psum.tile([P, C], F32, name="bank%d" % (e - 5))
+        for i, (s0, s1) in enumerate(spans[E - 2 :]):
+            bank = psum.tile([P, s1 - s0], F32, name="bank%d" % (E // 2 - 1 + i))
             sums.append(bank[:])
-        for e in range(E):
-            multiply(e, sums[e], [slot_words[(e, a)] for a in range(PASSES)], [slot_scales[(e, a)] for a in range(PASSES)])
-        for e in range(E):
-            nc.scalar.activation(y[:, e * C : (e + 1) * C], sums[e], GELU, bias=bias[:, e : e + 1])
+        for acc, (s0, s1) in zip(sums, spans):
+            multiply(s0 // C, acc, [slot_words[(s0, a)] for a in range(PASSES)], [slot_scales[(s0, a)] for a in range(PASSES)])
+        for acc, (s0, s1) in zip(sums, spans):
+            nc.scalar.activation(y[:, s0:s1], acc, GELU, bias=bias[:, s0 // C : s0 // C + 1])
 
-        pieces = ((0, 512, "bank7"), (512, T, "bank0"))
+        pieces = ((0, 512, "bank0"), (512, T, "bank1"))
         for lo, hi, tag in pieces:
             acc_shared = psum.tile([P, hi - lo], F32, name="acc_shared%d" % lo, tag=tag)
             multiply(
                 E,
                 acc_shared[:],
-                [tok_words[:, a * T + lo : a * T + hi] for a in range(PASSES)],
+                [tok_words[:, first_word(a) + lo : first_word(a) + hi] for a in range(PASSES)],
                 [tok_scales[4 * a : P, lo:hi] for a in range(PASSES)],
             )
             nc.scalar.activation(shared[:, lo:hi], acc_shared[:], GELU, bias=bias[:, E : E + 1])
@@ -191,7 +200,7 @@ def tile_moe_shr_lin_gelu_kernel(
             )
 
         blocks = T // P
-        turned_sums = [psum.tile([P, P], F32, name="turned_sum%d" % j, tag="bank%d" % (j + 1)) for j in range(blocks)]
+        turned_sums = [psum.tile([P, P], F32, name="turned_sum%d" % j, tag="bank%d" % (j + 2)) for j in range(blocks)]
 
         def add_turned(src, js, start, stop):
             for j in js:
@@ -204,9 +213,9 @@ def tile_moe_shr_lin_gelu_kernel(
         add_turned(shared, range(blocks), False, False)
         fetch(1, 0, T)
         add_turned(parts[1], range(blocks), False, False)
-        for j0 in (0, blocks // 2):
-            js = range(j0, j0 + blocks // 2)
-            fetch(2, js.start * P, js.stop * P)
+        for lo, hi, tag in pieces:
+            js = range(lo // P, hi // P)
+            fetch(2, lo, hi)
             add_turned(parts[2], js, False, True)
             for j in js:
                 nc.scalar.copy(turned[:, j * P : (j + 1) * P], turned_sums[j][:])

from contextlib import ExitStack

import concourse.mybir as mybir
from concourse.masks import make_identity

K, T, E, C, N = 1536, 768, 12, 256, 128
TOP = 4
S = E * C
FLOPS = 2 * K * N * (S + T)

F32 = mybir.dt.float32
BF16 = mybir.dt.bfloat16
I32 = mybir.dt.int32
U32 = mybir.dt.uint32
U16 = mybir.dt.uint16
U8 = mybir.dt.uint8
FP8X4 = mybir.dt.float8_e4m3fn_x4
GELU = mybir.ActivationFunctionType.Gelu_apprx_tanh
MULT = mybir.AluOpType.mult
ADD = mybir.AluOpType.add

P = 128
PACK = 4
PASSES = K // (P * PACK)
WIDE = 2048
HALF = S // 2
LANES = 16


def tile_moe_shr_lin_gelu_kernel(
    tc, x_words, x_scales, w, b, gate, offs, pos1, pos2, pos3, pos4, out
):
    nc = tc.nc
    with ExitStack() as ctx:
        lists = ctx.enter_context(tc.tile_pool(name="lists", bufs=1))
        held = ctx.enter_context(tc.tile_pool(name="held", bufs=1))
        psum = ctx.enter_context(tc.psum_pool(name="psum", bufs=1))

        slot_list = lists.tile([P, S // LANES], U16, name="slot_list")
        back_lists = [lists.tile([P, T // LANES], U16, name="back_list%d" % r) for r in range(TOP)]
        tok_words = held.tile([P, (PASSES - 1) * T + WIDE], I32, name="tok_words", align_bytes=64)
        tok_scales = held.tile([P, WIDE], U8, name="tok_scales", align_bytes=64)
        w_raw = [held.tile([P, PASSES, PACK, N], F32, name="w_raw%d" % e, tag="raw%d" % e, align_bytes=64) for e in range(E + 1)]
        w_bf = held.tile([P, (E + 1) * PASSES, N, PACK], BF16, name="w_bf", align_bytes=64)
        w_codes = held.tile([P, (E + 1) * PASSES * N], U32, name="w_codes", align_bytes=64)
        w_scales = held.tile([P, (E + 1) * PASSES * N], U8, name="w_scales", align_bytes=64)
        identity = held.tile([P, P], F32, name="identity")
        shared = held.tile([P, T], F32, name="shared")
        turned = held.tile([P, T], F32, name="turned")
        bias = held.tile([P, E + 1], F32, name="bias")
        gates = held.tile([P, TOP, T], F32, name="gates")
        y = held.tile([P, S], F32, name="y")
        total = held.tile([P, T], F32, name="total")
        parts = [held.tile([P, T], F32, name="part%d" % r) for r in range(TOP)]
        warm = held.tile([P, 1], F32, name="warm")
        warm_out = held.tile([P, 1], F32, name="warm_out")

        def first_word(a):
            return (PASSES - 1 - a) * T

        def load_words(a):
            nc.sync.dma_start(tok_words[:, first_word(a) : first_word(a) + T], x_words[a].rearrange("p t r -> p (t r)").bitcast(I32))

        def load_weight(e):
            nc.sync.dma_start(w_raw[e][:], w[e].rearrange("(a p j) n -> p a j n", a=PASSES, j=PACK))

        nc.vector.memset(warm[:], 0.0)
        nc.vector.memset(tok_words[:, PASSES * T :], 0)
        nc.vector.memset(tok_scales[:].bitcast(I32), 0)
        make_identity(nc, identity[:])
        nc.sync.dma_start(slot_list[:], offs)
        load_words(0)
        nc.scalar.activation(warm_out[:], warm[:], GELU)
        for e in range(E + 1):
            load_weight(e)
            if e == 1:
                for q in range(4):
                    nc.sync.dma_start(
                        tok_scales[32 * q : 32 * q + 4 * PASSES, 0:T].bitcast(I32),
                        x_scales[:, 4 * q : 4 * q + 4, :].bitcast(I32),
                    )
            if e == 2:
                load_words(1)
            if e == 4:
                load_words(2)
        nc.sync.dma_start(bias[:], b)
        for tile, pos in zip(back_lists, (pos1, pos2, pos3, pos4)):
            nc.sync.dma_start(tile[:], pos)
        for r in range(TOP):
            nc.sync.dma_start(gates[:, r, :], gate[r])

        def round_weight(e):
            nc.scalar.copy(
                w_bf[:, e * PASSES : (e + 1) * PASSES].rearrange("p a (c i) j -> p a c j i", i=4),
                w_raw[e][:].rearrange("p a j (c i) -> p a c j i", i=4),
            )

        w_flat = w_bf[:].rearrange("p a n j -> p (a n j)")

        def quantize(lo, hi):
            nc.vector.quantize_mx(
                out=w_codes[:, lo:hi].bitcast(FP8X4), scales=w_scales[:, lo:hi], in_=w_flat[:, PACK * lo : PACK * hi]
            )

        def multiply(e, acc, words, scales):
            for a in range(PASSES):
                cols = slice((e * PASSES + a) * N, (e * PASSES + a + 1) * N)
                nc.tensor.matmul_mx(
                    out=acc,
                    lhsT=w_codes[:, cols].bitcast(FP8X4),
                    lhsT_scale=w_scales[:, cols],
                    rhs=words[a].bitcast(FP8X4),
                    rhs_scale=scales[a],
                    start=(a == 0),
                    stop=(a == PASSES - 1),
                )

        def offsets(lo, hi):
            return slot_list[:, lo // LANES : hi // LANES]

        slot_words, slot_scales = {}, {}
        spans = [(e * C, (e + 1) * C) for e in range(E - 1)] + [(S - C, S - C // 2), (S - C // 2, S)]

        def gather_words(a, lo, hi, dst, width):
            window = tok_words[:, first_word(a) : first_word(a) + width].bitcast(U32)
            nc.vector.tensor_copy(dst, window.indirect(offsets(lo, hi)))
            for s0, s1 in spans:
                if lo <= s0 and s1 <= hi:
                    slot_words[(s0, a)] = dst[:, s0 - lo : s1 - lo]

        def gather_scales(lo, hi, tag):
            tile = held.tile([P, hi - lo], U8, name="slot_scales%d" % lo, tag=tag, align_bytes=64)
            nc.vector.tensor_copy(tile[:], tok_scales[:].indirect(offsets(lo, hi)))
            for s0, s1 in spans:
                if lo <= s0 and s1 <= hi:
                    for a in range(PASSES):
                        slot_scales[(s0, a)] = tile[4 * a : P, s0 - lo : s1 - lo]

        def words_tile(name, width, tag):
            return held.tile([P, width], U32, name=name, tag=tag, align_bytes=64)

        gather_words(0, 0, HALF, words_tile("words_0a", HALF, "words_0a")[:], WIDE)
        gather_words(0, HALF, S, words_tile("words_0b", HALF, "words_0b")[:], WIDE)
        step = WIDE // PACK
        done = 0
        for e in range(E + 1):
            round_weight(e)
            while e < E and done + step <= (e + 1) * PASSES * N:
                quantize(done, done + step)
                done += step
            tag = "raw%d" % e
            if e == 0:
                gather_scales(0, HALF, tag)
            if e == 1:
                gather_words(1, 0, HALF, words_tile("words_1a", HALF, tag)[:], WIDE)
            if e == 3:
                gather_words(2, 0, HALF, words_tile("words_2a", HALF, tag)[:], WIDE)
            if e == 6:
                gather_scales(HALF, S, tag)
            if e == 8:
                gather_words(2, HALF, 10 * C, words_tile("words_2b", 4 * C, tag)[:], WIDE)
            if e == 9:
                gather_words(1, HALF, 10 * C, words_tile("words_1b", 4 * C, tag)[:], WIDE)
            if e == 10:
                gather_words(1, 10 * C, S, words_tile("words_1c", 2 * C, tag)[:], T)
            if e == 11:
                last = words_tile("words_2c", 2 * C, tag)
                gather_words(2, 10 * C, 11 * C, last[:, 0:C], T)
                gather_words(2, S - C, S - C // 2, last[:, C : C + C // 2], T)
                gather_words(2, S - C // 2, S, last[:, C + C // 2 : 2 * C], T)
        quantize(done, done + 2 * N)
        quantize(done + 2 * N, done + 3 * N)

        sums = []
        for c in range(E // 2 - 1):
            bank = psum.tile([P, 2 * C], F32, name="bank%d" % c)
            sums += [bank[:, 0:C], bank[:, C : 2 * C]]
        for i, (s0, s1) in enumerate(spans[E - 2 :]):
            bank = psum.tile([P, s1 - s0], F32, name="bank%d" % (E // 2 - 1 + i))
            sums.append(bank[:])
        for acc, (s0, s1) in zip(sums, spans):
            multiply(s0 // C, acc, [slot_words[(s0, a)] for a in range(PASSES)], [slot_scales[(s0, a)] for a in range(PASSES)])
        for acc, (s0, s1) in zip(sums, spans):
            nc.scalar.activation(y[:, s0:s1], acc, GELU, bias=bias[:, s0 // C : s0 // C + 1])

        pieces = ((0, 512, "bank0"), (512, T, "bank1"))
        for lo, hi, tag in pieces:
            acc_shared = psum.tile([P, hi - lo], F32, name="acc_shared%d" % lo, tag=tag)
            multiply(
                E,
                acc_shared[:],
                [tok_words[:, first_word(a) + lo : first_word(a) + hi] for a in range(PASSES)],
                [tok_scales[4 * a : P, lo:hi] for a in range(PASSES)],
            )
            nc.scalar.activation(shared[:, lo:hi], acc_shared[:], GELU, bias=bias[:, E : E + 1])

        def fetch(r, lo, hi):
            nc.vector.tensor_tensor(
                parts[r][:, lo:hi], y[:].indirect(back_lists[r][:, lo // LANES : hi // LANES]), gates[:, r, lo:hi], MULT
            )

        blocks = T // P
        turned_sums = [psum.tile([P, P], F32, name="turned_sum%d" % j, tag="bank%d" % (j + 2)) for j in range(blocks)]

        def add_turned(src, js, start, stop):
            for j in js:
                nc.tensor.matmul(
                    turned_sums[j][:], src[:, j * P : (j + 1) * P], identity[:], start=start, stop=stop, is_transpose=True
                )

        fetch(0, 0, T)
        add_turned(parts[0], range(blocks), True, False)
        add_turned(shared, range(blocks), False, False)
        fetch(1, 0, T)
        add_turned(parts[1], range(blocks), False, False)
        for lo, hi, tag in pieces:
            js = range(lo // P, hi // P)
            fetch(2, lo, hi)
            add_turned(parts[2], js, False, True)
            for j in js:
                nc.scalar.copy(turned[:, j * P : (j + 1) * P], turned_sums[j][:])
        for lo, hi, tag in pieces:
            fetch(3, lo, hi)
        for lo, hi, tag in pieces:
            back = psum.tile([P, hi - lo], F32, name="back%d" % lo, tag=tag)
            for c0 in range(lo, hi, P):
                nc.tensor.transpose(back[:, c0 - lo : c0 - lo + P], turned[:, c0 : c0 + P], identity[:])
            nc.vector.tensor_tensor(total[:, lo:hi], back[:], parts[3][:, lo:hi], ADD)
            nc.sync.dma_start(out[:, lo:hi], total[:, lo:hi])
